import numpy as np
import ml_dtypes


def mxq(x, axis, fmt="e4m3"):
    dtype, down = {"e4m3": (ml_dtypes.float8_e4m3fn, 7), "e5m2": (ml_dtypes.float8_e5m2, 14)}[fmt]
    v = np.moveaxis(np.asarray(x, np.float32).astype(ml_dtypes.bfloat16).astype(np.float64), axis, -1)
    blocks = v.reshape(v.shape[:-1] + (-1, 32))
    amax = np.abs(blocks).max(-1, keepdims=True)
    byte = np.maximum(np.where(amax > 0, np.frexp(amax)[1] - 1 + 127, 0) - down, 1)
    scale = np.exp2(byte - 127.0)
    codes = (blocks / scale).astype(np.float32).astype(dtype).astype(np.float64)
    return np.moveaxis((codes * scale).reshape(v.shape), -1, axis)


WIDE = False


def mx_kscale(k):
    if not WIDE:
        return np.ones(k)
    levels = np.array([30, -30])
    if k % 512:
        return np.exp2(np.random.permutation(np.resize(levels, k // 32))).repeat(32)
    a = np.empty((k // 512, 16))
    for p in range(k // 512):
        a[p, :8] = np.random.permutation(np.resize(levels, 8))
        for g in range(8):
            far = levels[np.abs(levels - a[p, g]) >= 10]
            a[p, g + 8] = far[np.random.randint(len(far))]
    return np.exp2(a.ravel()).repeat(32)


def f64(x):
    return np.asarray(x).astype(np.float64)


def striped(idx):
    return np.tile(np.asarray(idx).reshape(-1, 16).T, (8, 1)).astype(np.uint16)


def unstriped(offs):
    return offs[:16].T.reshape(-1).astype(np.int64)


E2M1 = np.array([0.0, 0.5, 1.0, 1.5, 2.0, 3.0, 4.0, 6.0, -0.0, -0.5, -1.0, -1.5, -2.0, -3.0, -4.0, -6.0])


def pack_weight(w, fmt):
    k, n = w.shape
    w = f64(np.asarray(w, np.float32).astype(ml_dtypes.bfloat16)).reshape(k // 32, 32, n)
    amax = np.abs(w).max(1)
    if fmt in ("e4m3", "e5m2"):
        byte = np.frexp(amax)[1] - 1 + 127 - (7 if fmt == "e4m3" else 14)
    else:
        mant, ex = np.frexp(amax / 6.0)
        byte = np.where(mant > 0.5, ex, ex - 1) + 127
    byte = np.clip(np.where(amax > 0, byte, 1), 1, 254)
    scaled = (w * np.exp2(127.0 - byte)[:, None, :]).reshape(k, n).astype(np.float32)
    by_word = np.ascontiguousarray(scaled.reshape(k // 512, 128, 4, n).transpose(0, 1, 3, 2))
    if fmt in ("e4m3", "e5m2"):
        words = by_word.astype(ml_dtypes.float8_e4m3fn if fmt == "e4m3" else ml_dtypes.float8_e5m2).view(np.uint8)
    else:
        c = by_word.astype(ml_dtypes.float4_e2m1fn).view(np.uint8) & 0xF
        words = (c[..., 0::2] | (c[..., 1::2] << 4)).reshape(k // 512, 128, 2 * n)
    return np.ascontiguousarray(words), np.ascontiguousarray(byte.astype(np.uint8).reshape(k // 512, 16, n))


def unpack_weight(words, scales, fmt):
    g, _, n = scales.shape
    words = np.ascontiguousarray(words).reshape(g, 128, n, -1)
    if fmt in ("e4m3", "e5m2"):
        vals = words.view(ml_dtypes.float8_e4m3fn if fmt == "e4m3" else ml_dtypes.float8_e5m2).astype(np.float64)
    else:
        nib = np.empty((g, 128, n, 4), np.uint8)
        nib[..., 0::2] = words & 0xF
        nib[..., 1::2] = words >> 4
        vals = E2M1[nib]
    vals = vals * np.repeat(np.exp2(scales.astype(np.float64) - 127.0), 8, axis=1)[..., None]
    return vals.transpose(0, 1, 3, 2).reshape(g * 512, n)


def sigmoid(v):
    return 1.0 / (1.0 + np.exp(-v))


def sgn(shape):
    return np.random.uniform(0.5, 2.0, shape) * np.where(np.random.standard_normal(shape) < 0, -1.0, 1.0)


K, T, J, R, I, O, N, E = 512, 1024, 256, 512, 256, 128, 256, 512


def setup_inputs():
    n = np.random.standard_normal
    idx = np.random.permutation(T)[:J]
    idx2 = np.random.permutation(J)[:I]
    idx3 = np.random.permutation(J)[:I]
    idx4 = np.random.permutation(I)[:O]
    idx5 = np.random.permutation(I)[:O]
    idx6 = np.random.permutation(E)[:O]
    idx7 = np.random.permutation(E)[:O]
    fk = mx_kscale(K)
    fr = mx_kscale(R)
    xtp = pack_weight(n((K, T)) / fk[:, None], "e5m2")
    wp = pack_weight(n((K, R)) * 1 / np.sqrt(K) * fk[:, None], "e2m1")
    wbp = pack_weight(n((R, N)) * 1 / np.sqrt(R) / fr[:, None], "e2m1")
    return {
        "xt_words": xtp[0],
        "xt_scales": xtp[1],
        "w_words": wp[0],
        "w_scales": wp[1],
        "sa": (sgn((R, 1)) * fr[:, None]).astype(np.float32),
        "sg": (sgn((R, 1))).astype(np.float32),
        "bg": (np.random.uniform(-2.0, 2.0, (R, 1))).astype(np.float32),
        "wb_words": wbp[0],
        "wb_scales": wbp[1],
        "offs": striped(idx),
        "offs2": striped(idx2),
        "offs3": striped(idx3),
        "offs4": striped(idx4),
        "offs5": striped(idx5),
        "offs6": striped(idx6),
        "offs7": striped(idx7),
    }


def reference(xt_words, xt_scales, w_words, w_scales, sa, sg, bg, wb_words, wb_scales, offs, offs2, offs3, offs4, offs5, offs6, offs7):
    idx = unstriped(offs)
    idx2 = unstriped(offs2)
    idx3 = unstriped(offs3)
    idx4 = unstriped(offs4)
    idx5 = unstriped(offs5)
    idx6 = unstriped(offs6)
    idx7 = unstriped(offs7)
    xtu = unpack_weight(xt_words, xt_scales, "e5m2")
    wu = unpack_weight(w_words, w_scales, "e2m1")
    wbu = unpack_weight(wb_words, wb_scales, "e2m1")
    xtidxg = xtu[:, idx]
    a = wu.T @ xtidxg
    h1 = a[:, idx2] * f64(sa) * sigmoid(a[:, idx3] * f64(sg) + f64(bg))
    hid = np.maximum(h1[:, idx4], h1[:, idx5])
    hidq = mxq(hid, 0, "e4m3")
    p = wbu.T @ hidq
    pa = np.zeros((N, E))
    pa[:, idx6] = p
    pb = np.zeros((N, E))
    pb[:, idx7] = p
    y = pa + pb
    return y

@@ -1,0 +1,199 @@
+from contextlib import ExitStack
+
+import concourse.mybir as mybir
+
+K, T, J, R, I, O, N, E = 512, 1024, 256, 512, 256, 128, 256, 512
+FLOPS = 2 * K * R * J + 2 * R * N * O
+
+F32 = mybir.dt.float32
+BF16 = mybir.dt.bfloat16
+I32 = mybir.dt.int32
+U32 = mybir.dt.uint32
+U16 = mybir.dt.uint16
+U8 = mybir.dt.uint8
+E4M3X4 = mybir.dt.float8_e4m3fn_x4
+E5M2X4 = mybir.dt.float8_e5m2_x4
+E2M1X4 = mybir.dt.float4_e2m1fn_x4
+ACT = mybir.ActivationFunctionType
+ALU = mybir.AluOpType
+
+P = 128
+PACK = 4
+QUADS = 4
+QUAD = 32
+WINDOW = 2 * J
+
+
+def tile_list_gatedthenlook_solo_one_pagetwice_kernel(
+    tc, xt_words, xt_scales, w_words, w_scales, sa, sg, bg, wb_words, wb_scales,
+    offs, offs2, offs3, offs4, offs5, offs6, offs7, out,
+):
+    nc = tc.nc
+    with ExitStack() as ctx:
+        sb = ctx.enter_context(tc.tile_pool(name="sb", bufs=1))
+        ring = ctx.enter_context(tc.tile_pool(name="ring", bufs=2))
+        ps = ctx.enter_context(tc.psum_pool(name="ps", bufs=1))
+
+        def load_list(name, src):
+            tile = sb.tile([P, src.shape[1]], U16, name=name)
+            nc.sync.dma_start(tile[:], src)
+            return tile
+
+        def load_rows(name, src, queue):
+            tile = sb.tile([P, PACK], F32, name=name)
+            queue.dma_start(tile[:], src.rearrange("(p t) o -> p (t o)", t=PACK))
+            return tile
+
+        xs = sb.tile([P, T], U8, name="xs", align_bytes=64)
+        nc.vector.memset(xs[:].bitcast(I32), 0)
+        ws = sb.tile([P, R], U8, name="ws", align_bytes=64)
+        nc.vector.memset(ws[:].bitcast(I32), 0)
+        wbs = sb.tile([P, N], U8, name="wbs", align_bytes=64)
+        nc.vector.memset(wbs[:].bitcast(I32), 0)
+
+        xw = sb.tile([P, T], U32, name="xw", align_bytes=64)
+        l1 = load_list("l1", offs)
+        nc.sync.dma_start(xw[:].bitcast(I32), xt_words[0].rearrange("p c r -> p (c r)").bitcast(I32))
+        ws_stage = sb.tile([PACK, QUADS, R // 4], I32, name="ws_stage")
+        nc.scalar.dma_start(ws_stage[:], w_scales[0].bitcast(I32).rearrange("(q r) c -> r q c", r=PACK))
+        for q in range(QUADS):
+            nc.sync.dma_start(
+                xs[QUAD * q : QUAD * q + PACK, :].bitcast(I32),
+                xt_scales[0, PACK * q : PACK * (q + 1), :].bitcast(I32),
+            )
+        ww = sb.tile([P, R], U16, name="ww", align_bytes=64)
+        nc.sync.dma_start(ww[:].bitcast(I32), w_words[0].bitcast(I32))
+        l3 = load_list("l3", offs3)
+        l2 = load_list("l2", offs2)
+        sa_t = load_rows("sa_t", sa, nc.sync)
+        sg_t = load_rows("sg_t", sg, nc.sync)
+        bg_t = load_rows("bg_t", bg, nc.sync)
+        l4 = load_list("l4", offs4)
+        l5 = load_list("l5", offs5)
+        wbw = sb.tile([P, 2 * N], U8, name="wbw", align_bytes=64)
+        nc.sync.dma_start(wbw[:].bitcast(I32), wb_words[0].bitcast(I32))
+        for q in range(QUADS):
+            nc.sync.dma_start(
+                wbs[QUAD * q : QUAD * q + PACK, :].bitcast(I32),
+                wb_scales[0, PACK * q : PACK * (q + 1), :].bitcast(I32),
+            )
+        l6 = load_list("l6", offs6)
+        l7 = load_list("l7", offs7)
+
+        halves = N // P
+        page_a = [sb.tile([P, E], F32, name="page_a%d" % h) for h in range(halves)]
+        page_b = [sb.tile([P, E], F32, name="page_b%d" % h) for h in range(halves)]
+        for h in range(halves):
+            nc.vector.memset(page_a[h][:], 0.0)
+            nc.vector.memset(page_b[h][:], 0.0)
+
+        ww_by_t = ww[:].rearrange("p (m t) -> p t m", t=PACK)
+
+        for q in range(QUADS):
+            nc.vector.tensor_copy(ws[QUAD * q : QUAD * q + PACK, :].bitcast(I32), ws_stage[:, q, :])
+
+        xwg = sb.tile([P, J], U32, name="xwg", align_bytes=64)
+        nc.vector.tensor_copy(xwg[:], xw[:].indirect(l1[:]))
+        xsg = sb.tile([P, J], U8, name="xsg", align_bytes=64)
+        nc.vector.tensor_copy(xsg[:], xs[:].indirect(l1[:]))
+        ws_by_t = ws[:].rearrange("p (m t) -> p t m", t=PACK)
+        wsd0 = sb.tile([P, P], U8, name="wsd0", align_bytes=64)
+        nc.vector.tensor_copy(wsd0[:], ws_by_t[:, 0, :])
+        wd0 = sb.tile([P, P], U16, name="wd0", align_bytes=64)
+        nc.scalar.copy(wd0[:], ww_by_t[:, 0, :])
+        wsdr = sb.tile([P, PACK - 1, P], U8, name="wsdr", align_bytes=64)
+        nc.vector.tensor_copy(wsdr[:], ws_by_t[:, 1:PACK, :])
+        wdr = sb.tile([P, PACK - 1, P], U16, name="wdr", align_bytes=64)
+        nc.scalar.copy(wdr[:], ww_by_t[:, 1:PACK, :])
+
+        a_sb = []
+        for t in range(PACK):
+            acc = ps.tile([P, J], F32, name="acc%d" % t)
+            nc.tensor.matmul_mx(
+                out=acc[:],
+                lhsT=(wd0[:] if t == 0 else wdr[:, t - 1, :]).bitcast(E2M1X4),
+                lhsT_scale=wsd0[:] if t == 0 else wsdr[:, t - 1, :],
+                rhs=xwg[:].bitcast(E5M2X4),
+                rhs_scale=xsg[:],
+                start=True,
+                stop=True,
+            )
+            a_t = sb.tile([P, WINDOW], F32, name="a%d" % t)
+            if t == 0:
+                nc.scalar.copy(a_t[:, 0:J], acc[:])
+            else:
+                nc.vector.tensor_copy(a_t[:, 0:J], acc[:])
+            a_sb.append(a_t)
+
+        pick4 = sb.tile([P, PACK, O], F32, name="pick4")
+        pick5 = sb.tile([P, PACK, O], F32, name="pick5")
+        hid = sb.tile([P, O, PACK], BF16, name="hid", align_bytes=64)
+
+        def larger(t0):
+            nc.vector.tensor_tensor(
+                hid[:, :, t0 : t0 + 2],
+                pick4[:, t0 : t0 + 2, :].rearrange("p t o -> p o t"),
+                pick5[:, t0 : t0 + 2, :].rearrange("p t o -> p o t"),
+                ALU.max,
+            )
+
+        for t in range(PACK):
+            last = t == PACK - 1
+            gate = ring.tile([P, I], F32, name="gate")
+            nc.scalar.activation(
+                out=gate[:], in_=a_sb[t][:].indirect(l3[:]), func=ACT.Sigmoid,
+                bias=bg_t[:, t : t + 1], scale=sg_t[:, t : t + 1],
+            )
+            val = ring.tile([P, I], F32, name="val")
+            h1 = sb.tile([P, I], F32, name="h1_%d" % t)
+            parts = 2 if last else 1
+            width = I // parts
+            for u in range(parts):
+                cols = slice(u * width, (u + 1) * width)
+                nc.scalar.activation(
+                    out=val[:, cols],
+                    in_=a_sb[t][:].indirect(l2[:, u * width // 16 : (u + 1) * width // 16]),
+                    func=ACT.Copy, scale=sa_t[:, t : t + 1],
+                )
+                nc.vector.tensor_tensor(h1[:, cols], val[:, cols], gate[:, cols], ALU.mult)
+            if t == 2:
+                larger(0)
+            nc.vector.tensor_copy(pick4[:, t, :], h1[:].indirect(l4[:]))
+            if last:
+                nc.scalar.activation(out=pick5[:, t, :], in_=h1[:].indirect(l5[:]), func=ACT.Copy)
+            else:
+                nc.vector.tensor_copy(pick5[:, t, :], h1[:].indirect(l5[:]))
+        larger(2)
+
+        codes = sb.tile([P, O], U32, name="codes", align_bytes=64)
+        scales = sb.tile([P, O], U8, name="scales", align_bytes=64)
+        nc.vector.quantize_mx(
+            out=codes[:].bitcast(E4M3X4), scales=scales[:], in_=hid[:].rearrange("p o t -> p (o t)"),
+        )
+
+        p_sb = []
+        for h in range(halves):
+            res = ps.tile([P, O], F32, name="res%d" % h)
+            nc.tensor.matmul_mx(
+                out=res[:],
+                lhsT=wbw[:, 2 * P * h : 2 * P * (h + 1)].bitcast(E2M1X4),
+                lhsT_scale=wbs[:, P * h : P * (h + 1)],
+                rhs=codes[:].bitcast(E4M3X4),
+                rhs_scale=scales[:],
+                start=True,
+                stop=True,
+            )
+            p_h = sb.tile([P, O], F32, name="p%d" % h)
+            if h == 0:
+                nc.vector.tensor_copy(p_h[:], res[:])
+            else:
+                nc.scalar.copy(p_h[:], res[:])
+            p_sb.append(p_h)
+
+        for h in range(halves):
+            nc.scalar.activation(out=page_a[h][:].indirect(l6[:]), in_=p_sb[h][:], func=ACT.Copy)
+            nc.vector.tensor_copy(page_b[h][:].indirect(l7[:]), p_sb[h][:])
+        for h in range(halves):
+            total = sb.tile([P, E], F32, name="total%d" % h)
+            nc.vector.tensor_tensor(total[:], page_a[h][:], page_b[h][:], ALU.add)
+            nc.sync.dma_start(out[P * h : P * (h + 1), :], total[:])

@@ -80,6 +80,10 @@ def tile_list_gatedthenlook_solo_one_pagetwice_kernel(
         l6 = load_list("l6", offs6)
         l7 = load_list("l7", offs7)
 
+        cold = sb.tile([P, 1], F32, name="cold")
+        nc.gpsimd.memset(cold[:], 0.0)
+        warm = sb.tile([P, 1], F32, name="warm")
+        nc.scalar.activation(out=warm[:], in_=cold[:], func=ACT.Sigmoid)
         halves = N // P
         page_a = [sb.tile([P, E], F32, name="page_a%d" % h) for h in range(halves)]
         page_b = [sb.tile([P, E], F32, name="page_b%d" % h) for h in range(halves)]

@@ -21,7 +21,20 @@ P = 128
 PACK = 4
 QUADS = 4
 QUAD = 32
+LIVE = 4
+PER_COLUMN = 16
+MX_ALIGN = 64
 WINDOW = 2 * J
+HALVES = N // P
+
+
+def entries(lst, cols):
+    return lst[:, cols.start // PER_COLUMN : cols.stop // PER_COLUMN]
+
+
+def pieces(total, count):
+    width = total // count
+    return [slice(u * width, (u + 1) * width) for u in range(count)]
 
 
 def tile_list_gatedthenlook_solo_one_pagetwice_kernel(
@@ -35,48 +48,49 @@ def tile_list_gatedthenlook_solo_one_pagetwice_kernel(
         ps = ctx.enter_context(tc.psum_pool(name="ps", bufs=1))
 
         def load_list(name, src):
-            tile = sb.tile([P, src.shape[1]], U16, name=name)
-            nc.sync.dma_start(tile[:], src)
-            return tile
+            lst = sb.tile([P, src.shape[1]], U16, name=name)
+            nc.sync.dma_start(lst[:], src)
+            return lst
 
-        def load_rows(name, src, queue):
-            tile = sb.tile([P, PACK], F32, name=name)
-            queue.dma_start(tile[:], src.rearrange("(p t) o -> p (t o)", t=PACK))
-            return tile
+        def load_by_slice(name, src):
+            vec = sb.tile([P, PACK], F32, name=name)
+            nc.sync.dma_start(vec[:], src.rearrange("(p t) o -> p (t o)", t=PACK))
+            return vec
 
-        xs = sb.tile([P, T], U8, name="xs", align_bytes=64)
-        nc.vector.memset(xs[:].bitcast(I32), 0)
-        ws = sb.tile([P, R], U8, name="ws", align_bytes=64)
-        nc.vector.memset(ws[:].bitcast(I32), 0)
-        wbs = sb.tile([P, N], U8, name="wbs", align_bytes=64)
-        nc.vector.memset(wbs[:].bitcast(I32), 0)
+        def zeroed_scale_tile(name, columns):
+            scale_tile = sb.tile([P, columns], U8, name=name, align_bytes=MX_ALIGN)
+            nc.vector.memset(scale_tile[:].bitcast(I32), 0)
+            return scale_tile
 
-        xw = sb.tile([P, T], U32, name="xw", align_bytes=64)
+        def load_scale_rows(scale_tile, src):
+            for q in range(QUADS):
+                nc.sync.dma_start(
+                    scale_tile[QUAD * q : QUAD * q + LIVE, :].bitcast(I32),
+                    src[0, LIVE * q : LIVE * (q + 1), :].bitcast(I32),
+                )
+
+        xs = zeroed_scale_tile("xs", T)
+        ws = zeroed_scale_tile("ws", R)
+        wbs = zeroed_scale_tile("wbs", N)
+
+        xw = sb.tile([P, T], U32, name="xw", align_bytes=MX_ALIGN)
         l1 = load_list("l1", offs)
         nc.sync.dma_start(xw[:].bitcast(I32), xt_words[0].rearrange("p c r -> p (c r)").bitcast(I32))
-        ws_stage = sb.tile([PACK, QUADS, R // 4], I32, name="ws_stage")
-        nc.scalar.dma_start(ws_stage[:], w_scales[0].bitcast(I32).rearrange("(q r) c -> r q c", r=PACK))
-        for q in range(QUADS):
-            nc.sync.dma_start(
-                xs[QUAD * q : QUAD * q + PACK, :].bitcast(I32),
-                xt_scales[0, PACK * q : PACK * (q + 1), :].bitcast(I32),
-            )
-        ww = sb.tile([P, R], U16, name="ww", align_bytes=64)
+        ws_stage = sb.tile([LIVE, QUADS, R // 4], I32, name="ws_stage")
+        nc.scalar.dma_start(ws_stage[:], w_scales[0].bitcast(I32).rearrange("(q r) c -> r q c", r=LIVE))
+        load_scale_rows(xs, xt_scales)
+        ww = sb.tile([P, R], U16, name="ww", align_bytes=MX_ALIGN)
         nc.sync.dma_start(ww[:].bitcast(I32), w_words[0].bitcast(I32))
-        l3 = load_list("l3", offs3)
         l2 = load_list("l2", offs2)
-        sa_t = load_rows("sa_t", sa, nc.sync)
-        sg_t = load_rows("sg_t", sg, nc.sync)
-        bg_t = load_rows("bg_t", bg, nc.sync)
+        sa_t = load_by_slice("sa_t", sa)
+        l3 = load_list("l3", offs3)
+        sg_t = load_by_slice("sg_t", sg)
+        bg_t = load_by_slice("bg_t", bg)
         l4 = load_list("l4", offs4)
         l5 = load_list("l5", offs5)
-        wbw = sb.tile([P, 2 * N], U8, name="wbw", align_bytes=64)
+        wbw = sb.tile([P, 2 * N], U8, name="wbw", align_bytes=MX_ALIGN)
         nc.sync.dma_start(wbw[:].bitcast(I32), wb_words[0].bitcast(I32))
-        for q in range(QUADS):
-            nc.sync.dma_start(
-                wbs[QUAD * q : QUAD * q + PACK, :].bitcast(I32),
-                wb_scales[0, PACK * q : PACK * (q + 1), :].bitcast(I32),
-            )
+        load_scale_rows(wbs, wb_scales)
         l6 = load_list("l6", offs6)
         l7 = load_list("l7", offs7)
 
@@ -84,99 +98,95 @@ def tile_list_gatedthenlook_solo_one_pagetwice_kernel(
         nc.gpsimd.memset(cold[:], 0.0)
         warm = sb.tile([P, 1], F32, name="warm")
         nc.scalar.activation(out=warm[:], in_=cold[:], func=ACT.Sigmoid)
-        halves = N // P
-        page_a = [sb.tile([P, E], F32, name="page_a%d" % h) for h in range(halves)]
-        page_b = [sb.tile([P, E], F32, name="page_b%d" % h) for h in range(halves)]
-        for h in range(halves):
+
+        page_a = [sb.tile([P, E], F32, name="page_a%d" % h) for h in range(HALVES)]
+        page_b = [sb.tile([P, E], F32, name="page_b%d" % h) for h in range(HALVES)]
+        for h in range(HALVES):
             nc.vector.memset(page_a[h][:], 0.0)
             nc.vector.memset(page_b[h][:], 0.0)
 
-        ww_by_t = ww[:].rearrange("p (m t) -> p t m", t=PACK)
-
         for q in range(QUADS):
-            nc.vector.tensor_copy(ws[QUAD * q : QUAD * q + PACK, :].bitcast(I32), ws_stage[:, q, :])
+            nc.vector.tensor_copy(ws[QUAD * q : QUAD * q + LIVE, :].bitcast(I32), ws_stage[:, q, :])
 
-        xwg = sb.tile([P, J], U32, name="xwg", align_bytes=64)
-        nc.vector.tensor_copy(xwg[:], xw[:].indirect(l1[:]))
-        xsg = sb.tile([P, J], U8, name="xsg", align_bytes=64)
-        nc.vector.tensor_copy(xsg[:], xs[:].indirect(l1[:]))
+        ww_by_t = ww[:].rearrange("p (m t) -> p t m", t=PACK)
         ws_by_t = ws[:].rearrange("p (m t) -> p t m", t=PACK)
-        wsd0 = sb.tile([P, P], U8, name="wsd0", align_bytes=64)
+        wsd0 = sb.tile([P, P], U8, name="wsd0", align_bytes=MX_ALIGN)
         nc.vector.tensor_copy(wsd0[:], ws_by_t[:, 0, :])
-        wd0 = sb.tile([P, P], U16, name="wd0", align_bytes=64)
+        xwg = sb.tile([P, J], U32, name="xwg", align_bytes=MX_ALIGN)
+        xsg = sb.tile([P, J], U8, name="xsg", align_bytes=MX_ALIGN)
+        for cols in pieces(J, 2):
+            nc.vector.tensor_copy(xwg[:, cols], xw[:].indirect(entries(l1, cols)))
+            nc.vector.tensor_copy(xsg[:, cols], xs[:].indirect(entries(l1, cols)))
+        wd0 = sb.tile([P, P], U16, name="wd0", align_bytes=MX_ALIGN)
         nc.scalar.copy(wd0[:], ww_by_t[:, 0, :])
-        wsdr = sb.tile([P, PACK - 1, P], U8, name="wsdr", align_bytes=64)
+        wsdr = sb.tile([P, PACK - 1, P], U8, name="wsdr", align_bytes=MX_ALIGN)
         nc.vector.tensor_copy(wsdr[:], ws_by_t[:, 1:PACK, :])
-        wdr = sb.tile([P, PACK - 1, P], U16, name="wdr", align_bytes=64)
+        wdr = sb.tile([P, PACK - 1, P], U16, name="wdr", align_bytes=MX_ALIGN)
         nc.scalar.copy(wdr[:], ww_by_t[:, 1:PACK, :])
+        w_slices = [wd0[:]] + [wdr[:, t, :] for t in range(PACK - 1)]
+        ws_slices = [wsd0[:]] + [wsdr[:, t, :] for t in range(PACK - 1)]
 
         a_sb = []
         for t in range(PACK):
-            acc = ps.tile([P, J], F32, name="acc%d" % t)
-            nc.tensor.matmul_mx(
-                out=acc[:],
-                lhsT=(wd0[:] if t == 0 else wdr[:, t - 1, :]).bitcast(E2M1X4),
-                lhsT_scale=wsd0[:] if t == 0 else wsdr[:, t - 1, :],
-                rhs=xwg[:].bitcast(E5M2X4),
-                rhs_scale=xsg[:],
-                start=True,
-                stop=True,
-            )
+            first = t == 0
             a_t = sb.tile([P, WINDOW], F32, name="a%d" % t)
-            if t == 0:
-                nc.scalar.copy(a_t[:, 0:J], acc[:])
-            else:
-                nc.vector.tensor_copy(a_t[:, 0:J], acc[:])
+            for u, cols in enumerate(pieces(J, 2 if first else 1)):
+                acc = ps.tile([P, cols.stop - cols.start], F32, name="acc%d_%d" % (t, u))
+                nc.tensor.matmul_mx(
+                    out=acc[:],
+                    lhsT=w_slices[t].bitcast(E2M1X4),
+                    lhsT_scale=ws_slices[t],
+                    rhs=xwg[:, cols].bitcast(E5M2X4),
+                    rhs_scale=xsg[:, cols],
+                    start=True,
+                    stop=True,
+                )
+                if first:
+                    nc.scalar.copy(a_t[:, cols], acc[:])
+                else:
+                    nc.vector.tensor_copy(a_t[:, cols], acc[:])
             a_sb.append(a_t)
 
         pick4 = sb.tile([P, PACK, O], F32, name="pick4")
         pick5 = sb.tile([P, PACK, O], F32, name="pick5")
-        hid = sb.tile([P, O, PACK], BF16, name="hid", align_bytes=64)
-
-        def larger(t0):
-            nc.vector.tensor_tensor(
-                hid[:, :, t0 : t0 + 2],
-                pick4[:, t0 : t0 + 2, :].rearrange("p t o -> p o t"),
-                pick5[:, t0 : t0 + 2, :].rearrange("p t o -> p o t"),
-                ALU.max,
-            )
-
+        hid = sb.tile([P, O, PACK], BF16, name="hid", align_bytes=MX_ALIGN)
+        h1_sb = []
         for t in range(PACK):
             last = t == PACK - 1
-            gate = ring.tile([P, I], F32, name="gate")
-            nc.scalar.activation(
-                out=gate[:], in_=a_sb[t][:].indirect(l3[:]), func=ACT.Sigmoid,
-                bias=bg_t[:, t : t + 1], scale=sg_t[:, t : t + 1],
-            )
             val = ring.tile([P, I], F32, name="val")
+            nc.scalar.activation(
+                out=val[:], in_=a_sb[t][:].indirect(l2[:]), func=ACT.Copy, scale=sa_t[:, t : t + 1],
+            )
+            gate = ring.tile([P, I], F32, name="gate")
             h1 = sb.tile([P, I], F32, name="h1_%d" % t)
-            parts = 2 if last else 1
-            width = I // parts
-            for u in range(parts):
-                cols = slice(u * width, (u + 1) * width)
+            for cols in pieces(I, 2 if last else 1):
                 nc.scalar.activation(
-                    out=val[:, cols],
-                    in_=a_sb[t][:].indirect(l2[:, u * width // 16 : (u + 1) * width // 16]),
-                    func=ACT.Copy, scale=sa_t[:, t : t + 1],
+                    out=gate[:, cols], in_=a_sb[t][:].indirect(entries(l3, cols)),
+                    func=ACT.Sigmoid, bias=bg_t[:, t : t + 1], scale=sg_t[:, t : t + 1],
                 )
                 nc.vector.tensor_tensor(h1[:, cols], val[:, cols], gate[:, cols], ALU.mult)
-            if t == 2:
-                larger(0)
-            nc.vector.tensor_copy(pick4[:, t, :], h1[:].indirect(l4[:]))
+            h1_sb.append(h1)
+            if t > 0:
+                nc.vector.tensor_copy(pick5[:, t - 1, :], h1_sb[t - 1][:].indirect(l5[:]))
             if last:
                 nc.scalar.activation(out=pick5[:, t, :], in_=h1[:].indirect(l5[:]), func=ACT.Copy)
-            else:
-                nc.vector.tensor_copy(pick5[:, t, :], h1[:].indirect(l5[:]))
-        larger(2)
+            nc.vector.tensor_copy(pick4[:, t, :], h1[:].indirect(l4[:]))
 
-        codes = sb.tile([P, O], U32, name="codes", align_bytes=64)
-        scales = sb.tile([P, O], U8, name="scales", align_bytes=64)
+        for pair in pieces(PACK, 2):
+            nc.vector.tensor_tensor(
+                hid[:, :, pair],
+                pick4[:, pair, :].rearrange("p t o -> p o t"),
+                pick5[:, pair, :].rearrange("p t o -> p o t"),
+                ALU.max,
+            )
+        codes = sb.tile([P, O], U32, name="codes", align_bytes=MX_ALIGN)
+        scales = sb.tile([P, O], U8, name="scales", align_bytes=MX_ALIGN)
         nc.vector.quantize_mx(
             out=codes[:].bitcast(E4M3X4), scales=scales[:], in_=hid[:].rearrange("p o t -> p (o t)"),
         )
 
         p_sb = []
-        for h in range(halves):
+        for h in range(HALVES):
             res = ps.tile([P, O], F32, name="res%d" % h)
             nc.tensor.matmul_mx(
                 out=res[:],
@@ -194,10 +204,13 @@ def tile_list_gatedthenlook_solo_one_pagetwice_kernel(
                 nc.scalar.copy(p_h[:], res[:])
             p_sb.append(p_h)
 
-        for h in range(halves):
+        for h in range(HALVES):
             nc.scalar.activation(out=page_a[h][:].indirect(l6[:]), in_=p_sb[h][:], func=ACT.Copy)
             nc.vector.tensor_copy(page_b[h][:].indirect(l7[:]), p_sb[h][:])
-        for h in range(halves):
-            total = sb.tile([P, E], F32, name="total%d" % h)
-            nc.vector.tensor_tensor(total[:], page_a[h][:], page_b[h][:], ALU.add)
-            nc.sync.dma_start(out[P * h : P * (h + 1), :], total[:])
+
+        for h in range(HALVES):
+            for u, cols in enumerate(pieces(E, 2)):
+                total = sb.tile([P, E // 2], F32, name="total%d_%d" % (h, u))
+                adder = nc.gpsimd if (h, u) == (0, 0) else nc.vector
+                adder.tensor_tensor(total[:], page_a[h][:, cols], page_b[h][:, cols], ALU.add)
+                nc.sync.dma_start(out[P * h : P * (h + 1), cols], total[:])

@@ -75,12 +75,12 @@ def tile_list_gatedthenlook_solo_one_pagetwice_kernel(
 
         xw = sb.tile([P, T], U32, name="xw", align_bytes=MX_ALIGN)
         l1 = load_list("l1", offs)
-        nc.sync.dma_start(xw[:].bitcast(I32), xt_words[0].rearrange("p c r -> p (c r)").bitcast(I32))
         ws_stage = sb.tile([LIVE, QUADS, R // 4], I32, name="ws_stage")
         nc.scalar.dma_start(ws_stage[:], w_scales[0].bitcast(I32).rearrange("(q r) c -> r q c", r=LIVE))
-        load_scale_rows(xs, xt_scales)
+        nc.scalar.dma_start(xw[:].bitcast(I32), xt_words[0].rearrange("p c r -> p (c r)").bitcast(I32))
         ww = sb.tile([P, R], U16, name="ww", align_bytes=MX_ALIGN)
         nc.sync.dma_start(ww[:].bitcast(I32), w_words[0].bitcast(I32))
+        load_scale_rows(xs, xt_scales)
         l2 = load_list("l2", offs2)
         sa_t = load_by_slice("sa_t", sa)
         l3 = load_list("l3", offs3)
@@ -114,9 +114,9 @@ def tile_list_gatedthenlook_solo_one_pagetwice_kernel(
         nc.vector.tensor_copy(wsd0[:], ws_by_t[:, 0, :])
         xwg = sb.tile([P, J], U32, name="xwg", align_bytes=MX_ALIGN)
         xsg = sb.tile([P, J], U8, name="xsg", align_bytes=MX_ALIGN)
+        nc.vector.tensor_copy(xsg[:], xs[:].indirect(l1[:]))
         for cols in pieces(J, 2):
             nc.vector.tensor_copy(xwg[:, cols], xw[:].indirect(entries(l1, cols)))
-            nc.vector.tensor_copy(xsg[:, cols], xs[:].indirect(entries(l1, cols)))
         wd0 = sb.tile([P, P], U16, name="wd0", align_bytes=MX_ALIGN)
         nc.scalar.copy(wd0[:], ww_by_t[:, 0, :])
         wsdr = sb.tile([P, PACK - 1, P], U8, name="wsdr", align_bytes=MX_ALIGN)
@@ -211,6 +211,5 @@ def tile_list_gatedthenlook_solo_one_pagetwice_kernel(
         for h in range(HALVES):
             for u, cols in enumerate(pieces(E, 2)):
                 total = sb.tile([P, E // 2], F32, name="total%d_%d" % (h, u))
-                adder = nc.gpsimd if (h, u) == (0, 0) else nc.vector
-                adder.tensor_tensor(total[:], page_a[h][:, cols], page_b[h][:, cols], ALU.add)
+                nc.vector.tensor_tensor(total[:], page_a[h][:, cols], page_b[h][:, cols], ALU.add)
                 nc.sync.dma_start(out[P * h : P * (h + 1), cols], total[:])

from contextlib import ExitStack

import concourse.mybir as mybir

K, T, J, R, I, O, N, E = 512, 1024, 256, 512, 256, 128, 256, 512
FLOPS = 2 * K * R * J + 2 * R * N * O

F32 = mybir.dt.float32
BF16 = mybir.dt.bfloat16
I32 = mybir.dt.int32
U32 = mybir.dt.uint32
U16 = mybir.dt.uint16
U8 = mybir.dt.uint8
E4M3X4 = mybir.dt.float8_e4m3fn_x4
E5M2X4 = mybir.dt.float8_e5m2_x4
E2M1X4 = mybir.dt.float4_e2m1fn_x4
ACT = mybir.ActivationFunctionType
ALU = mybir.AluOpType

P = 128
PACK = 4
QUADS = 4
QUAD = 32
LIVE = 4
PER_COLUMN = 16
MX_ALIGN = 64
WINDOW = 2 * J
HALVES = N // P


def entries(lst, cols):
    return lst[:, cols.start // PER_COLUMN : cols.stop // PER_COLUMN]


def pieces(total, count):
    width = total // count
    return [slice(u * width, (u + 1) * width) for u in range(count)]


def tile_list_gatedthenlook_solo_one_pagetwice_kernel(
    tc, xt_words, xt_scales, w_words, w_scales, sa, sg, bg, wb_words, wb_scales,
    offs, offs2, offs3, offs4, offs5, offs6, offs7, out,
):
    nc = tc.nc
    with ExitStack() as ctx:
        sb = ctx.enter_context(tc.tile_pool(name="sb", bufs=1))
        ring = ctx.enter_context(tc.tile_pool(name="ring", bufs=2))
        ps = ctx.enter_context(tc.psum_pool(name="ps", bufs=1))

        def load_list(name, src):
            lst = sb.tile([P, src.shape[1]], U16, name=name)
            nc.sync.dma_start(lst[:], src)
            return lst

        def load_by_slice(name, src):
            vec = sb.tile([P, PACK], F32, name=name)
            nc.sync.dma_start(vec[:], src.rearrange("(p t) o -> p (t o)", t=PACK))
            return vec

        def zeroed_scale_tile(name, columns):
            scale_tile = sb.tile([P, columns], U8, name=name, align_bytes=MX_ALIGN)
            nc.vector.memset(scale_tile[:].bitcast(I32), 0)
            return scale_tile

        def load_scale_rows(scale_tile, src):
            for q in range(QUADS):
                nc.sync.dma_start(
                    scale_tile[QUAD * q : QUAD * q + LIVE, :].bitcast(I32),
                    src[0, LIVE * q : LIVE * (q + 1), :].bitcast(I32),
                )

        xs = zeroed_scale_tile("xs", T)
        ws = zeroed_scale_tile("ws", R)
        wbs = zeroed_scale_tile("wbs", N)

        xw = sb.tile([P, T], U32, name="xw", align_bytes=MX_ALIGN)
        l1 = load_list("l1", offs)
        ws_stage = sb.tile([LIVE, QUADS, R // 4], I32, name="ws_stage")
        nc.scalar.dma_start(ws_stage[:], w_scales[0].bitcast(I32).rearrange("(q r) c -> r q c", r=LIVE))
        nc.scalar.dma_start(xw[:].bitcast(I32), xt_words[0].rearrange("p c r -> p (c r)").bitcast(I32))
        ww = sb.tile([P, R], U16, name="ww", align_bytes=MX_ALIGN)
        nc.sync.dma_start(ww[:].bitcast(I32), w_words[0].bitcast(I32))
        load_scale_rows(xs, xt_scales)
        l2 = load_list("l2", offs2)
        sa_t = load_by_slice("sa_t", sa)
        l3 = load_list("l3", offs3)
        sg_t = load_by_slice("sg_t", sg)
        bg_t = load_by_slice("bg_t", bg)
        l4 = load_list("l4", offs4)
        l5 = load_list("l5", offs5)
        wbw = sb.tile([P, 2 * N], U8, name="wbw", align_bytes=MX_ALIGN)
        nc.sync.dma_start(wbw[:].bitcast(I32), wb_words[0].bitcast(I32))
        load_scale_rows(wbs, wb_scales)
        l6 = load_list("l6", offs6)
        l7 = load_list("l7", offs7)

        cold = sb.tile([P, 1], F32, name="cold")
        nc.gpsimd.memset(cold[:], 0.0)
        warm = sb.tile([P, 1], F32, name="warm")
        nc.scalar.activation(out=warm[:], in_=cold[:], func=ACT.Sigmoid)

        page_a = [sb.tile([P, E], F32, name="page_a%d" % h) for h in range(HALVES)]
        page_b = [sb.tile([P, E], F32, name="page_b%d" % h) for h in range(HALVES)]
        for h in range(HALVES):
            nc.vector.memset(page_a[h][:], 0.0)
            nc.vector.memset(page_b[h][:], 0.0)

        for q in range(QUADS):
            nc.vector.tensor_copy(ws[QUAD * q : QUAD * q + LIVE, :].bitcast(I32), ws_stage[:, q, :])

        ww_by_t = ww[:].rearrange("p (m t) -> p t m", t=PACK)
        ws_by_t = ws[:].rearrange("p (m t) -> p t m", t=PACK)
        wsd0 = sb.tile([P, P], U8, name="wsd0", align_bytes=MX_ALIGN)
        nc.vector.tensor_copy(wsd0[:], ws_by_t[:, 0, :])
        xwg = sb.tile([P, J], U32, name="xwg", align_bytes=MX_ALIGN)
        xsg = sb.tile([P, J], U8, name="xsg", align_bytes=MX_ALIGN)
        nc.vector.tensor_copy(xsg[:], xs[:].indirect(l1[:]))
        for cols in pieces(J, 2):
            nc.vector.tensor_copy(xwg[:, cols], xw[:].indirect(entries(l1, cols)))
        wd0 = sb.tile([P, P], U16, name="wd0", align_bytes=MX_ALIGN)
        nc.scalar.copy(wd0[:], ww_by_t[:, 0, :])
        wsdr = sb.tile([P, PACK - 1, P], U8, name="wsdr", align_bytes=MX_ALIGN)
        nc.vector.tensor_copy(wsdr[:], ws_by_t[:, 1:PACK, :])
        wdr = sb.tile([P, PACK - 1, P], U16, name="wdr", align_bytes=MX_ALIGN)
        nc.scalar.copy(wdr[:], ww_by_t[:, 1:PACK, :])
        w_slices = [wd0[:]] + [wdr[:, t, :] for t in range(PACK - 1)]
        ws_slices = [wsd0[:]] + [wsdr[:, t, :] for t in range(PACK - 1)]

        a_sb = []
        for t in range(PACK):
            first = t == 0
            a_t = sb.tile([P, WINDOW], F32, name="a%d" % t)
            for u, cols in enumerate(pieces(J, 2 if first else 1)):
                acc = ps.tile([P, cols.stop - cols.start], F32, name="acc%d_%d" % (t, u))
                nc.tensor.matmul_mx(
                    out=acc[:],
                    lhsT=w_slices[t].bitcast(E2M1X4),
                    lhsT_scale=ws_slices[t],
                    rhs=xwg[:, cols].bitcast(E5M2X4),
                    rhs_scale=xsg[:, cols],
                    start=True,
                    stop=True,
                )
                if first:
                    nc.scalar.copy(a_t[:, cols], acc[:])
                else:
                    nc.vector.tensor_copy(a_t[:, cols], acc[:])
            a_sb.append(a_t)

        pick4 = sb.tile([P, PACK, O], F32, name="pick4")
        pick5 = sb.tile([P, PACK, O], F32, name="pick5")
        hid = sb.tile([P, O, PACK], BF16, name="hid", align_bytes=MX_ALIGN)
        h1_sb = []
        for t in range(PACK):
            last = t == PACK - 1
            val = ring.tile([P, I], F32, name="val")
            nc.scalar.activation(
                out=val[:], in_=a_sb[t][:].indirect(l2[:]), func=ACT.Copy, scale=sa_t[:, t : t + 1],
            )
            gate = ring.tile([P, I], F32, name="gate")
            h1 = sb.tile([P, I], F32, name="h1_%d" % t)
            for cols in pieces(I, 2 if last else 1):
                nc.scalar.activation(
                    out=gate[:, cols], in_=a_sb[t][:].indirect(entries(l3, cols)),
                    func=ACT.Sigmoid, bias=bg_t[:, t : t + 1], scale=sg_t[:, t : t + 1],
                )
                nc.vector.tensor_tensor(h1[:, cols], val[:, cols], gate[:, cols], ALU.mult)
            h1_sb.append(h1)
            if t > 0:
                nc.vector.tensor_copy(pick5[:, t - 1, :], h1_sb[t - 1][:].indirect(l5[:]))
            if last:
                nc.scalar.activation(out=pick5[:, t, :], in_=h1[:].indirect(l5[:]), func=ACT.Copy)
            nc.vector.tensor_copy(pick4[:, t, :], h1[:].indirect(l4[:]))

        for pair in pieces(PACK, 2):
            nc.vector.tensor_tensor(
                hid[:, :, pair],
                pick4[:, pair, :].rearrange("p t o -> p o t"),
                pick5[:, pair, :].rearrange("p t o -> p o t"),
                ALU.max,
            )
        codes = sb.tile([P, O], U32, name="codes", align_bytes=MX_ALIGN)
        scales = sb.tile([P, O], U8, name="scales", align_bytes=MX_ALIGN)
        nc.vector.quantize_mx(
            out=codes[:].bitcast(E4M3X4), scales=scales[:], in_=hid[:].rearrange("p o t -> p (o t)"),
        )

        p_sb = []
        for h in range(HALVES):
            res = ps.tile([P, O], F32, name="res%d" % h)
            nc.tensor.matmul_mx(
                out=res[:],
                lhsT=wbw[:, 2 * P * h : 2 * P * (h + 1)].bitcast(E2M1X4),
                lhsT_scale=wbs[:, P * h : P * (h + 1)],
                rhs=codes[:].bitcast(E4M3X4),
                rhs_scale=scales[:],
                start=True,
                stop=True,
            )
            p_h = sb.tile([P, O], F32, name="p%d" % h)
            if h == 0:
                nc.vector.tensor_copy(p_h[:], res[:])
            else:
                nc.scalar.copy(p_h[:], res[:])
            p_sb.append(p_h)

        for h in range(HALVES):
            nc.scalar.activation(out=page_a[h][:].indirect(l6[:]), in_=p_sb[h][:], func=ACT.Copy)
            nc.vector.tensor_copy(page_b[h][:].indirect(l7[:]), p_sb[h][:])

        for h in range(HALVES):
            for u, cols in enumerate(pieces(E, 2)):
                total = sb.tile([P, E // 2], F32, name="total%d_%d" % (h, u))
                nc.vector.tensor_tensor(total[:], page_a[h][:, cols], page_b[h][:, cols], ALU.add)
                nc.sync.dma_start(out[P * h : P * (h + 1), cols], total[:])
